import numpy as np, ml_dtypes
CORES = [7,15,23,39,47,63,71,79,87,95,119,127]
N = 12
TK = 64
def setup_inputs(rng):
    return {"x": rng.standard_normal((N, 128, N * TK), dtype=np.float32).astype(ml_dtypes.bfloat16), "t": rng.standard_normal((N, 128, N * TK), dtype=np.float32).astype(ml_dtypes.bfloat16), "f1": (rng.standard_normal((N, 128, 128), dtype=np.float32) / 11).astype(ml_dtypes.bfloat16), "f2": (rng.standard_normal((N, 128, 128), dtype=np.float32) / 11).astype(ml_dtypes.bfloat16)}
def setup_inputs_big(rng):
    d = setup_inputs(rng)
    for k in ("x", "t", "f1", "f2"): d[k] = (d[k].astype(np.float32) * 1024.0).astype(d[k].dtype)
    return d
def setup_inputs_small(rng):
    d = setup_inputs(rng)
    for k in ("x", "t", "f1", "f2"): d[k] = (d[k].astype(np.float32) * (1 / 1024.0)).astype(d[k].dtype)
    return d
def reference(x, t, f1, f2):
    X, T, F1, F2 = x.astype(np.float64), t.astype(np.float64), f1.astype(np.float64), f2.astype(np.float64)
    y = np.zeros((N, 128, N * TK))
    for j in range(N):
        u = (F1[j].T @ X[j]) * T[j]
        for r in range(N):
            y[r][:, TK * j:TK * j + TK] = F2[r].T @ u[:, TK * r:TK * r + TK]
    return {"y": y.astype(ml_dtypes.bfloat16)}

from concourse.bass import DstId, RemoteDMATransfer
from concourse.mybir import AluOpType

N = 12
BW = 64
STEPS = [("direct", 1, 2, 4), ("direct", 1, 4, 2), ("direct", 1, 4, 2), ("direct", 1, 1, 8)]
HELPER_ENGINES = 2
ORDER = [0, 1, 2, 3]
K = len(STEPS)
BANKS = 8


def _ranges():
    out, a = [], 0
    for _kind, w, n, _e in STEPS:
        out.append((a, a + w * n))
        a += w * n
    return out


RNG = _ranges()

SCRATCH = {
    "f1s": ("sbuf", [128, 128], "bfloat16"),
    "f2s": ("sbuf", [128, 128], "bfloat16"),
    "xs": ("sbuf", [128, N * BW], "bfloat16"),
    "ts": ("sbuf", [128, N * BW], "bfloat16"),
    "us": ("sbuf", [128, N * BW], "bfloat16"),
    "land": ("sbuf", [128, N * BW], "bfloat16"),
    "ys": ("sbuf", [128, N * BW], "bfloat16"),
    "stg": ("sbuf", [128, N * BW], "bfloat16"),
}
for _b in range(BANKS):
    SCRATCH["ps%d" % _b] = ("psum", [128, 512], "float32")

SEMAPHORES = ["lf1", "lf2", "own", "sent", "stg"]
for _k in range(K):
    SEMAPHORES += [s % _k for s in ("lx%d", "lt%d", "mm%d", "vv%d", "arr%d", "m2%d", "v2%d", "st%d")]


def _c(b):
    return b * BW


def _runs(first, count):
    first %= N
    if first + count <= N:
        return [(0, first, count)]
    k = N - first
    return [(0, first, k), (k, 0, count - k)]


def _engines(topo, src, dst):
    m = topo.mask(src, dst)
    return [e for e in range(16) if (m >> e) & 1]


def _transfer(topo, src_core, dst_core, src, dst, first, count, sem):
    rid, pid, _se = topo.addr(dst_core)
    mask = 0
    for e in _engines(topo, src_core, dst_core)[first:first + count]:
        mask |= 1 << e
    return RemoteDMATransfer(dst_ids=[DstId(rid=rid, pnc=pid)], dma_engine_mask=mask, remote_sem=sem, src=src, dst=dst)


def _helpers(owner, T, topo):
    cand = []
    for h in range(topo.CHIPS * topo.CORES_PER_CHIP):
        if h == owner or topo.chip(h) != topo.chip(owner) or T.rank_of(h) is not None:
            continue
        if all(topo.may_write(h, d) for d in T.cores):
            cand.append(h)
    return sorted(cand, key=lambda h: (topo.die(h) == topo.die(owner), h))


def _block_to(topo, T, src_core, rank, p, src, first, count, sem):
    d = (rank + 1 + p) % N
    q = N - 2 - p
    return _transfer(topo, src_core, T.cores[d], src, T.land[:, _c(q):_c(q + 1)], first, count, sem)


def _helper_program(g, core, T, topo):
    owners = [c for c in T.cores if topo.chip(c) == topo.chip(core)]
    if not owners:
        return
    hs = _helpers(owners[0], T, topo)
    rank = T.rank_of(owners[0])
    for k, (kind, w, n, e) in enumerate(STEPS):
        if kind != "relay" or core not in hs[:n]:
            continue
        i = hs.index(core)
        g.wait_ge(T.sem.stg, e)
        trs = [_block_to(topo, T, core, rank, RNG[k][0] + i * w + b, T.stg[:, _c(b):_c(b + 1)],
                         b * HELPER_ENGINES, HELPER_ENGINES, T.sem["arr%d" % k]) for b in range(w)]
        g.remote_dma_fused(trs, local_sem=T.sem.sent)
        g.wait_ge(T.sem.sent, w * HELPER_ENGINES)


def rank_program(g, core, T, topo):
    rank = T.rank_of(core)
    if rank is None:
        _helper_program(g, core, T, topo)
        return
    S = T.sem
    grp = [(a, b if k < K - 1 else N) for k, (a, b) in enumerate(RNG)]

    g.sync.dma_start(T.f1s[:], T.f1[:]).then_inc(S.lf1, 16)
    nld = []
    for k, (a, b) in enumerate(grp):
        runs = _runs(rank + 1 + a, b - a)
        for off, nat, ln in runs:
            g.scalar.dma_start(T.xs[:, _c(a + off):_c(a + off + ln)], T.x[:, _c(nat):_c(nat + ln)]).then_inc(S["lx%d" % k], 16)
            g.sync.dma_start(T.ts[:, _c(a + off):_c(a + off + ln)], T.t[:, _c(nat):_c(nat + ln)]).then_inc(S["lt%d" % k], 16)
        nld.append(16 * len(runs))
    g.scalar.dma_start(T.f2s[:], T.f2[:]).then_inc(S.lf2, 16)

    g.tensor.wait_ge(S.lf1, 16)
    for k, (a, b) in enumerate(grp):
        ps = T["ps%d" % k]
        g.tensor.wait_ge(S["lx%d" % k], nld[k])
        g.tensor.matmul(ps[:, 0:_c(b - a)], T.f1s[:], T.xs[:, _c(a):_c(b)], start=True, stop=True).then_inc(S["mm%d" % k], 1)
        g.vector.wait_ge(S["mm%d" % k], 1)
        g.vector.wait_ge(S["lt%d" % k], nld[k])
        b1 = RNG[k][1]
        g.vector.tensor_tensor(T.us[:, _c(a):_c(b1)], ps[:, 0:_c(b1 - a)], T.ts[:, _c(a):_c(b1)],
                               op=AluOpType.mult).then_inc(S["vv%d" % k], 1)
    a = grp[K - 1][0]
    g.vector.tensor_tensor(T.land[:, _c(N - 1):_c(N)], T["ps%d" % (K - 1)][:, _c(N - 1 - a):_c(N - a)],
                           T.ts[:, _c(N - 1):_c(N)], op=AluOpType.mult).then_inc(S.own, 1)

    helpers = _helpers(core, T, topo)
    total = 0
    for k, (kind, w, n, e) in enumerate(STEPS):
        g.wait_ge(S["vv%d" % k], 1)
        a = RNG[k][0]
        trs = []
        for i in range(n):
            if kind == "direct":
                trs.append(_block_to(topo, T, core, rank, a + i, T.us[:, _c(a + i):_c(a + i + 1)], i * e, e, S["arr%d" % k]))
            else:
                trs.append(_transfer(topo, core, helpers[i], T.us[:, _c(a + i * w):_c(a + (i + 1) * w)],
                                     T.stg[:, 0:_c(w)], i * e, e, S.stg))
            total += e
        g.remote_dma_fused(trs, local_sem=S.sent)

    g.tensor.wait_ge(S.lf2, 16)
    stores = []
    for idx, k in enumerate(ORDER):
        kind, w, n, e = STEPS[k]
        a, b = RNG[k]
        q0, q1 = N - 1 - b, N - 1 - a
        bank = K + idx
        if bank >= BANKS:
            bank -= BANKS
            g.tensor.wait_ge(S["vv%d" % bank], 1)
            if bank == K - 1:
                g.tensor.wait_ge(S.own, 1)
        ps = T["ps%d" % bank]
        g.tensor.wait_ge(S["arr%d" % k], w * n * (e if kind == "direct" else HELPER_ENGINES))
        if a == 0:
            q1 = N
            g.tensor.wait_ge(S.own, 1)
        g.tensor.matmul(ps[:, 0:_c(q1 - q0)], T.f2s[:], T.land[:, _c(q0):_c(q1)], start=True, stop=True).then_inc(S["m2%d" % k], 1)
        g.vector.wait_ge(S["m2%d" % k], 1)
        g.vector.tensor_copy(T.ys[:, _c(q0):_c(q1)], ps[:, 0:_c(q1 - q0)]).then_inc(S["v2%d" % k], 1)
        queue = g.sync if idx % 2 == 0 else g.scalar
        queue.wait_ge(S["v2%d" % k], 1)
        runs = _runs(rank + 1 + q0, q1 - q0)
        for off, nat, ln in runs:
            queue.dma_start(T.y[:, _c(nat):_c(nat + ln)], T.ys[:, _c(q0 + off):_c(q0 + off + ln)]).then_inc(S["st%d" % k], 16)
        stores.append((queue, S["st%d" % k], 16 * len(runs)))
    for queue, sem, cnt in stores:
        queue.wait_ge(sem, cnt)
    g.wait_ge(S.sent, total)
